import numpy as np, ml_dtypes
CORES = [16,17,18,19,32,33,34,35]
N = 8
BF = ml_dtypes.bfloat16
def gentries(a):
    return np.ascontiguousarray(a.reshape(8, 16, -1).transpose(0, 2, 1)).reshape(8, -1)
def gtable(e):
    e = np.asarray(e); return np.ascontiguousarray(e.reshape(8, -1, 16).transpose(0, 2, 1)).reshape(128, -1).astype(np.int32)
W, E, P = 2048, 512, 5
M = (P - 1) // 2
def lens(rng, n, rw, how):
    i = np.arange(n)
    if how == 0: v = i % (P + 1)
    elif how == 1: v = np.where(i < (W - n - rw * (2 + M)) // ((P + 1) // 2), P, 0)
    elif how == 2: v = np.where(i % 10 < 9, 0, 1 + (i // 10) % P)
    elif how == 3: v = i % 3
    else: v = np.full(n, 1)
    return rng.permutation(v)
def colours(rng, ln, lo, hi):
    n = len(ln); a = rng.integers(lo, hi, n); b = lo + (a - lo + rng.integers(1, hi - lo, n)) % (hi - lo)
    x, y = np.maximum(a, b), np.minimum(a, b); z = ln == 0; same = rng.random(n) < 0.5
    return np.where(z, x, a), np.where(z, np.where(same, x, y), b)
def special(rng, rw):
    kd = (np.arange(rw) + rng.integers(0, 7)) % 7; q = rng.random(rw) < 0.5
    s = np.sort(np.argsort(rng.random((rw, 16)), axis=1)[:, :3], axis=1); j = rng.integers(0, 3, rw)
    j = np.where(kd == 0, 2, np.where((kd == 1) | (kd == 5), j % 2, j))
    s = np.take_along_axis(s, np.array([[2, 0, 1], [1, 0, 2], [0, 1, 2]])[j], axis=1)
    add, mul, span = np.array([[2, 2, 1, 1, 3, 0, 2], [2, 1, 2, 1, 1, 1, 1], [M, 1, 2, 4, 2, 1, 3]])[:, kd]
    return kd, q, s[:, 0], s[:, 1], s[:, 2], add + mul * (span * rng.random(rw)).astype(np.int64)
def way(v, ln, pl, pr):
    X = np.full((len(ln), P + 1), -1); X[:, 0] = v
    for i in range(1, P + 1):
        m = ln >= i; n = int(np.count_nonzero(m))
        if i % 2: X[m, i] = pl[:n]; pl = pl[n:]
        else: X[m, i] = pr[:n]; pr = pr[n:]
    return X, pl, pr
def plant(LT, RT, X, ln, a, b):
    for i in range(1, P + 1):
        m = ln >= i; p, x = X[m, i - 1], X[m, i]
        if i % 2: c = a[m]; RT[c, p] = x; LT[c, x] = p
        else: c = b[m]; LT[c, p] = x; RT[c, x] = p
    e = X[np.arange(len(ln)), ln]; m = ln % 2 == 0
    RT[a[m], e[m]] = -1; LT[b[~m], e[~m]] = -1
def graph(rng, rw, H, how, drop, order):
    LT = np.full((16, W), -2); RT = np.full((16, W), -2); LM = np.zeros((16, W), bool); RM = np.zeros((16, W), bool)
    C = np.arange(16)[:, None]; F = E - rw; S = E // 8
    if order == 0: nl, nr = rng.permutation(W), rng.permutation(W)
    elif order == 1: nl, nr = np.arange(W), np.arange(W)
    else: nl, nr = np.arange(W)[::-1], np.arange(W)[::-1]
    kd, q, a0, b0, e, l0 = special(rng, rw)
    ln = np.concatenate([l0, lens(rng, F, rw, how)])
    a, b = colours(rng, ln, 0, H); a[:rw] = a0; b[:rw] = b0
    u, v = nl[:E], nr[:E]; X, zl, zr = way(v, ln, nl[E:], nr[E:])
    plant(LT, RT, X, ln, a, b)
    LT[a, u] = -1; RT[b, v] = -1; LM[:, u] = C < a; RM[:, v] = C < b
    u0, v0, Z = u[:rw], v[:rw], X[:rw]; end = Z[np.arange(rw), l0]
    ua, zl = zl[:rw], zl[rw:]; zz, zr = zr[:rw], zr[rw:]
    m = (kd == 5) & q; n = int(np.count_nonzero(m)); p = np.array(ua); p[m] = zl[:n]; zl = zl[n:]
    c = np.where((kd == 3) | ((kd == 4) & q), b0, np.where(m | (kd == 6), e, a0))
    d = np.where((kd >= 2) & (kd <= 4), e, np.where((kd == 6) & q, a0, b0))
    y = np.where(kd < 2, end, np.where(kd == 4, Z[:, 2], np.where(kd == 6, zz, v0))); u1 = np.where(kd == 2, end, ua)
    s = np.where(kd == 3, Z[:, 1], np.where(kd == 4, np.where(q, Z[:, 3], Z[:, 1]), np.where(m, p, u0)))
    LM[:, u1] = C < c; RM[:, y] = C < d
    i = kd != 2; LT[c[i], ua[i]] = -1
    i = kd > 1; RT[d[i], y[i]] = -1
    i = (kd > 0) & (kd < 6); LT[d[i], s[i]] = zz[i]; RT[d[i], zz[i]] = s[i]; RT[c[i], zz[i]] = -1
    RT[e[m], v0[m]] = p[m]; LT[e[m], p[m]] = v0[m]
    i = kd == 6; x = Z[i, 1]; RT[e[i], zz[i]] = x; LT[e[i], x] = zz[i]; RT[e[i], np.where(q, Z[:, 2], v0)[i]] = -1
    i = kd == 0; LT[b0[i], u0[i]] = -1
    pu = rng.permutation(np.concatenate([u[rw:], zl[:S]])); pv = rng.permutation(np.concatenate([v[rw:], zr[:S]]))
    u2, v2 = pu[:F], pv[:F]; tl, tr = X[rw:, 1::2], X[rw:, 2::2]
    restl = rng.permutation(np.concatenate([pu[F:], zl[S:], tl[tl >= 0]])); restr = rng.permutation(np.concatenate([pv[F:], zr[S:], tr[tr >= 0]]))
    still = np.zeros(W, bool); still[v[(ln == 0) & (a > b)]] = True; z = still[v2]; g = ~z
    l2 = lens(rng, F, rw, how); l2[z] = 0
    c, d = colours(rng, l2, H, 16); Y, _, _ = way(v2, l2, restl, restr)
    plant(LT, RT, Y, l2, c, d)
    LT[c, u2] = -1; LM[:, u2] = LM[:, u2] | (C < c)
    RT[d[g], v2[g]] = -1; RM[:, v2[g]] = RM[:, v2[g]] | (C < d[g])
    for k in range(16):
        x, w = np.flatnonzero(LT[k] == -2), np.flatnonzero(RT[k] == -2); n = min(len(x), len(w))
        x = x[np.argsort(rng.random(len(x)) - 2.0 * LM[k, x])][:n]; w = rng.permutation(w[np.argsort(rng.random(len(w)) - 2.0 * RM[k, w])][:n])
        keep = LM[k, x] | RM[k, w] | (rng.random(n) >= drop); x, w = x[keep], w[keep]
        LT[k, x] = w; RT[k, w] = x
    k1 = rng.permutation(E) if order == 0 else np.arange(E); k2 = rng.permutation(E)
    return np.where(LT < 0, W, LT), np.where(RT < 0, W, RT), np.stack([u[k1], np.concatenate([u1, u2])[k2]]), np.stack([v[k1], np.concatenate([y, v2])[k2]])
def make(rng, pick):
    lt = np.zeros((N, 128, W), np.int32); rt = np.zeros((N, 128, W), np.int32); eu = np.zeros((N, 8, 2, E), np.int64); ev = np.zeros((N, 8, 2, E), np.int64)
    for q in range(N):
        for g in range(8):
            s = slice(16 * g, 16 * g + 16)
            lt[q, s], rt[(q + 1) % N, s], eu[q, g], ev[q, g] = graph(rng, *pick(q, g))
    return {"lt": lt, "rt": rt, "eu": np.stack([gtable(x.reshape(8, -1)) for x in eu]), "ev": np.stack([gtable(x.reshape(8, -1)) for x in ev])}
def setup_inputs(rng):
    return make(rng, lambda q, g: (E // 8, int(rng.integers(6, 11)), 0, 0.3 * rng.random(), 0))
def setup_inputs_again(rng):
    return make(rng, lambda q, g: (E // 4, int(rng.integers(6, 11)), 3, 0.3 * rng.random(), 0))
def setup_inputs_long(rng):
    return make(rng, lambda q, g: (0 if (q + g) % 4 == 3 else E // 8, int(rng.integers(6, 11)), 4 if (q + g) % 4 == 3 else 1, 0.3 * rng.random(), 0))
def setup_inputs_order(rng):
    return make(rng, lambda q, g: (E // 8, int(rng.integers(6, 11)), 0, 1.0 if g % 4 < 2 else 0.5, 1 + g % 2))
def setup_inputs_short(rng):
    return make(rng, lambda q, g: (E // 8, int(rng.integers(6, 11)), 2, 0.3 * rng.random(), 0))
def setup_inputs_spread(rng):
    return make(rng, lambda q, g: (int(rng.choice(np.array([1, E // 8]))), int(rng.integers(4, 13)), int(rng.integers(0, 4)), rng.random(), 0))
def load_all(lt, rt, eu, ev):
    none = np.full((8 * N, 16, 1), W, np.int64)
    L = np.concatenate([lt.astype(np.int64).reshape(8 * N, 16, W), none], axis=2)
    R = np.concatenate([np.roll(rt, -1, axis=0).astype(np.int64).reshape(8 * N, 16, W), none], axis=2)
    U, V = [np.stack([gentries(x) for x in t]).astype(np.int64).reshape(8 * N, 2, E) for t in (eu, ev)]
    return L, R, U, V
def turn(L, R, u, v):
    k = np.arange(8 * N)[:, None]
    fu = L[k, :, u] == W; fv = R[k, :, v] == W
    a = np.argmax(fu, axis=2); b = np.argmax(fv, axis=2); free = bool(np.all(np.any(fu, axis=2)) and np.all(np.any(fv, axis=2)))
    xs = [v]
    for i in range(P + 1):
        T = R if i % 2 == 0 else L; x = xs[-1]
        p, q = T[k, a, x], T[k, b, x]
        xs.append(p if i % 2 == 0 else q)
        T[k, a, x] = q; T[k, b, x] = p
    L[k, a, u] = v; R[k, a, v] = u
    return a, free, xs
def check_inputs(d):
    bad = []
    for k, hi in (("lt", W), ("rt", W), ("eu", W - 1), ("ev", W - 1)):
        if np.min(d[k]) < 0 or np.max(d[k]) > hi: bad.append("range of " + k)
    if bad: return bad
    L, R, U, V = load_all(d["lt"], d["rt"], d["eu"], d["ev"]); own = np.arange(W + 1)
    for A, B in ((L, R), (R, L)):
        if np.any((A < W) & (np.take_along_axis(B, A, 2) != own)): bad.append("lt and rt tell the same edges")
    if bad: return bad
    for t in range(2):
        a, free, xs = turn(L, R, U[:, t], V[:, t])
        if not free: bad.append("a free colour at both ends")
        if np.any(xs[P + 1] < W): bad.append("paths of at most P edges")
        for side in ([U[:, t]] + xs[1:P + 1:2], xs[0:P + 1:2]):
            s = np.sort(np.concatenate(side, axis=1), axis=1)
            if np.any((s[:, 1:] == s[:, :-1]) & (s[:, 1:] < W)): bad.append("different vertices in a round")
        if bad: return bad
    return bad
def reference(lt, rt, eu, ev):
    L, R, U, V = load_all(lt, rt, eu, ev); got = []
    for t in range(2):
        a, free, xs = turn(L, R, U[:, t], V[:, t]); got.append(a)
    return {"yl": np.ascontiguousarray(L[:, :, :W]).reshape(N, 128, W).astype(np.float32), "ya": np.concatenate(got, axis=1).reshape(N, 8, 2 * E).astype(np.float32)}

from concourse.mybir import AluOpType as ALU, AxisListType as AX, ActivationFunctionType as AF

W = 2048
E = 512
WIN = 2688
BIG = 8192.0
RCH = [0, 256, 640, 1024, 1536, 2048]
LCH = [0, 896, 1664, 2048]
OCH = [0, 256, 768, 1408, 2048]
NR, NL, NO = len(RCH) - 1, len(LCH) - 1, len(OCH) - 1
SEND = {False: [0, 1, 3, 4, 5], True: [0, 1, 2, 3, 4, 5]}
GATE = {False: [-1, -1, -1], True: [0, 1, 2]}
COLS = {False: 3, True: 2}
HANDED = [0, 1, 2]
F32, F16, BF, I32, U16 = "float32", "float16", "bfloat16", "int32", "uint16"

SCRATCH = {}
for _c, _d, _s in ((W, I32, "rt32 lt32"), (W, F16, "r16o r16i"), (WIN, F32, "LW RW"), (W, F32, "outb"), (128, I32, "e32"), (128, U16, "e16"),
                   (320, U16, "lst"), (160, F32, "m1 m2"), (128, F32, "KM KB tk tk2 OBf I32"), (128, F16, "OB NOB I16"), (1, F32, "pm hb"),
                   (128, BF, "OBW NOBb TR0 TRI BI NBI"), (32, F32, "fr32"), (32, F16, "FR"), (96, I32, "si32"), (96, U16, "SI"), (32, U16, "vin"),
                   (8, BF, "CW"), (288, F16, "Z"), (2 * E, F32, "yas"), (E, F16, "cvo cvi GV0 GV1 GU AU G1 G2 G3 G4 G5"),
                   (E, BF, "JM DM Fu Fv A0 B0 A1 B1 D Bx"), (E, F32, "colu col1 col3 col5 Pu P0 P1 P2 P3 P4 P5 w0 w2 w4 z0 z2 z4")):
    for _n in _s.split():
        SCRATCH[_n] = ("sbuf", [128, _c], _d)
for _i in range(8):
    SCRATCH["ps%d" % _i] = ("psum", [128, E], F32)

SEMAPHORES = (["qV", "qA", "qP", "qG", "sent", "dev", "deu", "dya", "arv", "arc"] + [s + str(k) for s in ("drt", "arr") for k in range(NR)]
              + ["dlt%d" % k for k in range(NL)] + ["dout%d" % k for k in range(NO)])

ORDER = {
    (False, False):
        "gU cL0 pR0 cv aR0 gV1 pR2 cL2 Fu0a.I cL1 Fu0b f02 tA0a A0a.V k0u mU f01 pR3 pR1 tA0b A0b pV gV0 aR1 Fv0 m0u tB0 AU G01 l01 vR4 c01 B0 mD G02 "
        "P0u md01 s0ub me01 m01 aR2 aR3 l02 Bx c02 mf01 G03 s0ua D m00 P00 md02 f03 l03 c03 me02 k03 w0 m02 mf02 z0 G04 md03 m03 P01 P03 f04 l04 c04 "
        "me03 mf03 r0a P02 md04 G05 k01 m04 f05 P04 w2 l05 m05 s01a r0b z2 c05 md05 s03b w4 me05 P05 k05 r2 s01b y0 z4 mf05 s03a f11 me04 mf04 s05 r4 "
        "f12 Fu1a.V Fu1b tA1b tA1a A1a.V A1b m1u G11 Fv1.S tB1 l11 c11 P1u B1.S k1u G12 md11 m11 l12 s1ua c12 Y0 me11 mf11 f13 f14 P11 y1 G13 l13 s1ub "
        "c13 Y1 G14 m13 k11 P13 md13 s11 l14 me13 c14 k13 dy mf13 G15 m15 s13 f15 l15 ma15 P15 c15 mb15 k15a k15b mc15 s15",
    (False, True):
        "gV1 cL0 gV0 gU mU cv f02 f01 cL1 cL2 pV Fu0b Fu0a.I Fv0 tA0a A0a.V tA0b A0b m0u tB0 k0u G01 l01 B0 P0u AU c01 G02 mD s0ub pR0 pR3 l02 Bx pR1 "
        "md01 m01 aR3 c02 s0ua md02 aR0 vR4 aR1 pR2 me01 aR2 mf01 G03 D m00 P01 me02 P00 k01 f03 l03 w0 c03 z0 m02 md03 mf02 me03 f04 G04 s01b r0b l04 "
        "c04 P02 mf03 G05 m03 k03 m04 w2 P03 md04 P04 f05 me04 r0a l05 mf04 z2 f12 s03a c05 m05 k05 w4 md05 r2 z4 me05 P05 s03b mf05 s01a r4 s05 Fu1a.V "
        "Fu1b y0 k1u tA1a tA1b A1b A1a.V G11 Fv1.S f11 m1u P1u tB1 l11 s1ub c11 B1.S G12 k11 md11 s1ua m11 l12 me11 c12 Y0 y1 mf11 f13 f14 G13 l13 P11 "
        "Y1 s11a c13 G14 k13 s11b m13 md13 l14 c14 me13 mf13 m15 P13 G15 f15 s13 l15 ma15 P15 c15 mb15 k15a k15b mc15 dy s15",
    (True, False):
        "pR1 gU cv f01 pR3 aR1 gV0 mU cL0 cL1 pR2 pR0 f02 gV1 aR3 cL2 Fu0a.I vR4 Fu0b aR0 tA0a tA0b A0b pV A0a.V m0u Fv0 G01 AU tB0 l01 k0u c01 B0 P0u "
        "md01 mD G02 Bx aR2 me01 mf01 s0ub m01 l02 m00 D c02 md02 P00 G03 me02 s0ua f03 l03 mf02 c03 md03 m02 k03 me03 P02 w0 G04 z0 f04 P01 l04 w2 c04 "
        "k01 z2 m03 mf03 G05 md04 r0a P03 m04 s03 me04 f05 P04 r2b l05 c05 m05 mf04 w4 md05 me05 y0 k05 P05 r2a s01 z4 mf05 s05 r0b r4 f11 Fu1a.V Fu1b "
        "tA1b tA1a A1a.V A1b m1u Fv1.S P1u G11 tB1 B1.S l11 c11 k1u y1 G12 md11 s1ua f12 me11 l12 Y0 c12 mf11 m11 G13 s1ub f13 P11 l13 c13 k11 f14 G14 "
        "Y1 m13 P13 dy s11 l14 md13 me13 k13 c14 mf13 m15 G15 s13 P15 f15 l15 ma15 c15 mb15 k15a k15b mc15 s15",
}


def bits(m):
    return bin(m).count("1")


def route(T, topo, src, dst):
    via = [None] * NR
    if topo.chip(src) != topo.chip(dst):
        free = [c for c in topo.cores_of(src) if T.rank_of(c) is None and topo.die(c) != topo.die(src) and topo.may_write(c, dst)]
        for k, c in zip(HANDED, free):
            via[k] = c
    return via


def helper_program(g, core, T, topo):
    n = len(T.cores)
    for r in range(n):
        src, dst = T.cores[(r + 1) % n], T.cores[r]
        for k, h in enumerate(route(T, topo, src, dst)):
            if h == core:
                a, b = RCH[k], RCH[k + 1]
                rid, pid, _ = topo.addr(dst)
                g.wait_ge(T.sem["arr%d" % k], bits(topo.mask(src, h) & ~topo.mask(src, dst)))
                g.remote_dma(T.r16i[:, a:b], T.r16i[:, a:b], T.sem["arr%d" % k], T.sem.sent, pid, rid, topo.mask(core, dst))
                g.wait_ge(T.sem.sent, bits(topo.mask(core, dst)))


def rank_program(g, core, T, topo):
    rank = T.rank_of(core)
    if rank is None:
        helper_program(g, core, T, topo)
        return
    n = len(T.cores)
    dst, src = T.cores[(rank - 1) % n], T.cores[(rank + 1) % n]
    far_out, far_in = topo.chip(core) != topo.chip(dst), topo.chip(core) != topo.chip(src)
    Q = {"V": g.vector, "A": g.scalar, "P": g.tensor, "G": g, "S": g.sync}
    V, A, P = g.vector, g.scalar, g.tensor
    known = {q: {} for q in Q}
    total, res, bank = {}, {}, {}
    idle = ["ps%d" % i for i in range(2, 8)]

    def need(q, tok):
        s, c, clock = tok
        k = known[q]
        if k.get(s, 0) < c:
            Q[q].wait_ge(T.sem[s], c)
            k[s] = c
            for s2, c2 in clock.items():
                k[s2] = max(k.get(s2, 0), c2)

    def order(q, reads, writes):
        toks = []
        for key in reads:
            r = res.get(key)
            if r is not None:
                toks += r["w"] + [t for q2, t in r["r"].items() if q2 != q and key.startswith("ps")]
        for key in writes:
            r = res.get(key)
            if r is not None:
                toks += ([] if q == "P" and r["wq"] == "P" else r["w"]) + list(r["r"].values())
        for t in sorted(toks, key=lambda t: -t[1]):
            need(q, t)

    def mark(q, tok, reads, writes):
        for key in reads:
            res.setdefault(key, {"w": [], "wq": None, "r": {}})["r"][q] = tok
        for key in writes:
            res[key] = {"w": [tok], "wq": q, "r": {}}

    def op(q, call, reads, writes):
        order(q, reads, writes)
        s = "q" + q
        total[s] = total.get(s, 0) + 1
        call().then_inc(T.sem[s], 1)
        mark(q, (s, total[s], dict(known[q])), reads, writes)

    def dma(q, s, out, in_, reads, writes):
        order(q, reads, writes)
        total[s] = 16
        Q[q].dma_start(out, in_).then_inc(T.sem[s], 16)
        mark(s, (s, 16, dict(known[q])), reads, writes)

    def send(to, out, in_, key, s, m):
        rid, pid, _ = topo.addr(to)
        order("G", [key], [])
        g.remote_dma(out, in_, T.sem[s], T.sem.sent, pid, rid, m)
        total["sent"] = total.get("sent", 0) + bits(m)

    def landed(keys, s, frm):
        total[s] = bits(topo.mask(frm, core))
        for key in keys:
            res[key] = {"w": [(s, total[s], {})], "wq": None, "r": {}}

    def act(out, in_, func, reads, writes, bias=0.0, scale=1.0):
        op("A", lambda: A.activation(out, in_, func, bias=bias, scale=scale), reads, writes)

    TAB = {t: [t + str(k) for k in range(NR)] + [t + "n"] for t in ("LW", "RW")}
    LISTS = {"v0": ("e16", 0), "v1": ("e16", 32), "u0": ("e16", 64), "u1": ("e16", 96)}
    for i in range(1, 6):
        LISTS["x%d" % i], LISTS["y%d" % i] = ("lst", 32 * (i - 1)), ("lst", 160 + 32 * (i - 1))

    def hk(name, h=None):
        return [name + ":0", name + ":1"] if h is None else [name + ":%d" % h]

    def cols(h):
        return (0, E) if h is None else (h * E // 2, (h + 1) * E // 2)

    def buf(name, h=None):
        return T[name][:, cols(h)[0]:cols(h)[1]]

    def offs(name, h=None):
        b, c = LISTS[name]
        return T[b][:, c + cols(h)[0] // 16:c + cols(h)[1] // 16]

    def lk(name):
        return ["e16"] if name[0] in "uv" else ["l" + name]

    def gat(tab, name, h=None):
        return T[tab][:, 0:W + 1].indirect(offs(name, h))

    def sca(tab, name, h=None):
        return T[tab][:, 0:WIN].indirect(offs(name, h))

    def take(use, readers=1):
        bank[use] = [idle.pop(0), readers]
        return bank[use][0]

    def give(use):
        bank[use][1] -= 1
        if bank[use][1] == 0:
            idle.append(bank[use][0])
        return bank[use][0]

    out = [RCH[i] for i in SEND[far_out]]
    gate = GATE[far_out or far_in]

    def load_left(k, reads):
        for j in range(NL):
            if gate[j] == k:
                dma("S", "dlt%d" % j, T.lt32[:, LCH[j]:LCH[j + 1]], T.lt[:, LCH[j]:LCH[j + 1]], reads, ["lt32:%d" % j])

    dma("A", "dev", T.e32[:, 0:64], T.ev[:, :], [], ["e32v"])
    dma("A", "deu", T.e32[:, 64:128], T.eu[:, :], [], ["e32u"])
    for k in range(len(out) - 1):
        dma("S", "drt%d" % k, T.rt32[:, out[k]:out[k + 1]], T.rt[:, out[k]:out[k + 1]], [], ["rt32:%d" % k])
    load_left(-1, [])

    def iota(name, pattern, base, cm):
        if SCRATCH[name][2] == I32:
            op("G", lambda: g.iota(T[name][:, :], pattern, base, cm), [], [name])
        else:
            op("G", lambda: g.iota(T[name][:, :], pattern, base, cm, allow_small_or_imprecise_dtypes=True), [], [name])

    def ts(out, in_, s, alu, more=()):
        op("V", lambda: V.tensor_scalar(T[out][:, :], T[in_][:, :], s, None, alu), [in_] + list(more), [out])

    def cp(out, in_, reads, writes):
        op("V", lambda: V.tensor_copy(out, in_), reads, writes)

    iota("KB", [[-16, 8], [0, 16]], 0, 1)
    iota("KM", [[-1, 128]], 0, 1)
    iota("si32", [[1, 96]], 0, 0)
    iota("fr32", [[16, 32]], 1, 1)
    iota("JM", [[0, 32], [1, 16]], 0, 0)
    op("V", lambda: V.memset(T.LW[:, W:W + 1], float(W)), [], ["LWn"])
    op("V", lambda: V.memset(T.RW[:, W:W + 1], float(W)), [], ["RWn"])
    op("V", lambda: V.memset(T.Z[:, :], 0.0), [], ["Z"])
    act(T.tk[:, :], T.KB[:, :], AF.Abs, ["KB"], ["tk"], bias=-7.5)
    act(T.tk2[:, :], T.KM[:, :], AF.Abs, ["KM"], ["tk2"])
    ts("OBf", "tk", 8.0, ALU.is_lt)
    ts("I16", "KM", 0.0, ALU.is_equal)
    act(T.BI[:, :], T.tk2[:, :], AF.Silu, ["tk2"], ["BI"], bias=BIG, scale=-2.0 * BIG)
    op("V", lambda: V.tensor_tensor(T.CW[:, :], T.KB[:, 0:128:16], T.OBf[:, 0:128:16], ALU.mult), ["KB", "OBf"], ["CW"])
    cp(T.OB[:, :], T.OBf[:, :], ["OBf"], ["OB"])
    op("V", lambda: V.tensor_reduce(T.pm[:, :], T.CW[:, :], AX.X, ALU.add), ["CW"], ["pm"])
    ts("NOB", "OBf", -1.0, ALU.mult)
    cp(T.Z[:, 15:143:16], T.OBf[:, 0:128:16], ["OBf", "Z"], ["Z0"])
    cp(T.Z[:, 160:288:16], T.OBf[:, 0:128:16], ["OBf", "Z"], ["Z1"])
    act(T.NOBb[:, :], T.OBf[:, :], AF.Identity, ["OBf"], ["NOBb"], scale=-1.0)
    act(T.OBW[:, :], T.OBf[:, :], AF.Identity, ["OBf"], ["OBW"], scale=float(W))
    act(T.I32[:, :], T.BI[:, :], AF.Identity, ["BI"], ["I32"], scale=1.0 / BIG)
    act(T.hb[:, :], T.pm[:, :], AF.Identity, ["pm"], ["hb"], scale=-0.5, bias=0.5)
    act(T.NBI[:, :], T.BI[:, :], AF.Identity, ["BI"], ["NBI"], scale=-1.0)

    cp(T.e16[:, 0:64], T.e32[:, 0:64], ["e32v"], ["e16v"])
    send(src, T.vin[:, :], T.e16[:, 0:32], "e16v", "arv", topo.mask(core, src))
    via, later = route(T, topo, core, dst), []
    for k in range(len(out) - 1):
        a, b = out[k], out[k + 1]
        cp(T.r16o[:, a:b], T.rt32[:, a:b], ["rt32:%d" % k], ["r16o:%d" % k])
        to = dst if via[k] is None else via[k]
        m = topo.mask(core, dst) if via[k] is None else topo.mask(core, to) & ~topo.mask(core, dst)
        later.append((to, T.r16i[:, a:b], T.r16o[:, a:b], "r16o:%d" % k, "arr%d" % k, m))
        if k <= COLS[far_out]:
            send(*later.pop())
        load_left(k, ["r16o:%d" % k])
    cp(T.SI[:, :], T.si32[:, :], ["si32"], ["SI"])
    ts("DM", "JM", T.pm[:, :], ALU.is_equal, ["pm"])
    cp(T.e16[:, 64:128], T.e32[:, 64:128], ["e32u", "e16v"], ["e16"])
    ts("FR", "fr32", 1.0 / W, ALU.mult)
    op("G", lambda: g.affine_select(T.TR0[:, :], T.NOBb[:, :], [[1, 128]], ALU.is_gt, 0.0, 0, -1), ["NOBb"], ["TR0"])
    op("G", lambda: g.affine_select(T.TRI[:, :], T.TR0[:, :], [[1, 128]], ALU.not_equal, 1.0, 0, -1), ["TR0"], ["TRI"])
    landed(["vin"], "arv", dst)
    landed(["cvi"], "arc", src)
    for k, h in enumerate(route(T, topo, src, core)[:len(SEND[far_in]) - 1]):
        landed(["r16i:%d" % j for j in range(SEND[far_in][k], SEND[far_in][k + 1])], "arr%d" % k, src if h is None else h)

    def mm(use, terms, readers=1, h=None):
        b = take(use, readers)
        for i, (l, r) in enumerate(terms):
            op("P", lambda: P.matmul(buf(b, h), T[l][:, :], buf(r, h), i == 0, i == len(terms) - 1), [l] + hk(r, h), [b])

    def fromps(out, use, bias=0.0, scale=1.0, func=AF.Relu, h=None, more=()):
        b = give(use)
        act(buf(out, h), buf(b, h), func, [b] + list(more), hk(out, h), bias=bias, scale=scale)

    def withps(out, use, other, alu):
        b = give(use)
        op("V", lambda: V.tensor_tensor(buf(out), buf(b), buf(other), alu), [b] + hk(other), hk(out))

    def wide(tab, s, ch, k):
        cp(T[tab][:, ch[k]:ch[k + 1]], T[s][:, ch[k]:ch[k + 1]], [s + ":%d" % k], [tab + str(k)])

    def free_v(window, keys, name, h):
        op("V", lambda: V.tensor_scalar(buf("Fu", h), window.indirect(offs(name, h)), W - 0.5, None, ALU.is_ge), keys + lk(name), hk("Fu", h))

    def spare(i, part):
        b, c = "ps%d" % (i % 2), 32 * (i - 1)
        ps, m1, m2 = T[b][:, 0:32], T.m1[:, c:c + 32], T.m2[:, c:c + 32]
        if part == "a":
            op("V", lambda: V.tensor_scalar(m1, ps, W - 1.0, float(W), ALU.subtract, ALU.mult), [b], ["m1%d" % i])
        elif part == "b":
            op("V", lambda: V.tensor_tensor(m2, ps, m1, ALU.max), [b, "m1%d" % i], ["m2%d" % i])
        elif part == "c":
            cp(offs("y%d" % i), m2, ["m2%d" % i], ["ly%d" % i])
        elif part == "d":
            act(m1, ps, AF.Relu, [b, "lx%d" % i], ["m1%d" % i], bias=-float(W * W), scale=float(W))
            act(m2, ps, AF.Identity, [b], ["m2%d" % i])
        elif part == "e":
            op("P", lambda: P.matmul(T[b][:, 32:64], T.I32[:, :], m1, True, False), ["I32", "m1%d" % i, "m2%d" % i], [b])
            op("P", lambda: P.matmul(T[b][:, 32:64], T.I32[:, :], m2, False, True), ["I32", "m2%d" % i], [b])
        else:
            cp(offs("y%d" % i), T[b][:, 32:64], [b], ["ly%d" % i])

    MASKS0, MASKS1 = [("BI", "A0"), ("BI", "B0")], [("BI", "A1"), ("BI", "B1")]
    SUMS = {"mU": [("OB", "GU")], "mD": [("BI", "A0"), ("NBI", "B0")],
            "tA0": [("TRI", "Fu")], "tB0": [("TRI", "Fv")], "tA1": [("TRI", "Fu")], "tB1": [("TRI", "Fv")],
            "m0u": [("NOB", "GV0"), ("BI", "A0")], "m1u": [("NOB", "GV1"), ("BI", "A1")],
            "m00": [("I16", "AU"), ("BI", "A0"), ("OB", "G1"), ("BI", "Bx")],
            "m02": MASKS0 + [("OB", "G1"), ("OB", "G3")], "m04": MASKS0 + [("OB", "G3"), ("OB", "G5")],
            "m01": [("NOB", "GV0"), ("OB", "G2")], "m03": [("NOB", "G2"), ("OB", "G4")], "m05": [("OBW", "B0"), ("NOB", "G4")],
            "m11": MASKS1 + [("OB", "GV1"), ("OB", "G2")], "m13": MASKS1 + [("OB", "G2"), ("OB", "G4")], "m15": MASKS1 + [("OB", "G4")]}

    def do(s):
        s, _, q = s.partition(".")
        h = {"a": 0, "b": 1}.get(s[-1])
        t, x = s[1:2], s[2:3]
        if s[:3] in SUMS:
            mm(s, SUMS[s[:3]], 2 if s == "mD" else 1, h)
        elif s == "cv":
            cp(T.cvo[:, :], T.rt32[:, :].indirect(T.vin[:, :]), ["rt32:%d" % j for j in range(len(out) - 1)] + ["vin"], ["cvo"])
            send(dst, T.cvi[:, :], T.cvo[:, :], "cvo", "arc", topo.mask(core, dst))
            for w in later:
                send(*w)
        elif s == "pV":
            b = take("cv", 3)
            op("P", lambda: P.matmul(T[b][:, :], T.I16[:, :], T.cvi[:, :], True, True), ["I16", "cvi"], [b])
        elif s == "Fv0":
            fromps("Fv", "cv", bias=1.0 - W)
        elif s == "G01":
            withps("G1", "cv", "A0", ALU.mult)
        elif s == "w0":
            withps("w0", "cv", "P0", ALU.subtract)
        elif s[0] == "g":
            c = {"gV0": 0, "gV1": 32, "gU": 64}[s]
            op("V", lambda: V.tensor_tensor(buf("G" + s[1:]), T.e32[:, :].indirect(T.SI[:, c:c + 32]), T.DM[:, :], ALU.mult),
               ["e32v", "e32u", "SI", "DM"], hk("G" + s[1:]))
        elif s[:2] == "cL":
            wide("LW", "lt32", LCH, int(x))
        elif s[:2] == "vR":
            wide("RW", "r16i", RCH, int(x))
        elif s[:2] == "pR":
            a, e, b = RCH[int(x)], RCH[int(x) + 1], take("R" + x)
            op("P", lambda: P.matmul(T[b][:, 0:e - a], T.I16[:, :], T.r16i[:, a:e], True, True), ["I16", "r16i:" + x], [b])
        elif s[:2] == "aR":
            a, e, b = RCH[int(x)], RCH[int(x) + 1], give("R" + x)
            act(T.RW[:, a:e], T[b][:, 0:e - a], AF.Identity, [b], ["RW" + x])
        elif s[:2] == "Fu":
            if q == "I":
                free_v(T.lt32[:, :], ["lt32:%d" % j for j in range(NL)], "u" + x, h)
            elif q == "V":
                free_v(T.LW[:, 0:W + 1], TAB["LW"], "u" + x, h)
            else:
                act(buf("Fu", h), gat("LW", "u" + x, h), AF.Relu, TAB["LW"] + lk("u"), hk("Fu", h), bias=1.0 - W)
        elif s == "Fv1":
            act(buf("Fv"), gat("RW", "v1"), AF.Sign, TAB["RW"] + lk("v"), hk("Fv"), bias=0.5 - W)
        elif s[:2] in ("A0", "A1", "B0", "B1"):
            if q == "V":
                b = give("t" + s)
                op("V", lambda: V.tensor_scalar(buf(s[:2], h), buf(b, h), 0.0, None, ALU.max), [b], hk(s[:2], h))
            elif q == "S":
                fromps(s[:2], "t" + s, bias=T.hb[:, :], scale=0.5, h=h, more=["hb"])
            else:
                fromps(s[:2], "t" + s, h=h)
        elif s == "AU":
            withps("AU", "mU", "A0", ALU.mult)
        elif s == "Bx":
            fromps("Bx", "mD", scale=-1.25 / BIG)
        elif s == "D":
            fromps("D", "mD", scale=1.0 / BIG, func=AF.Identity)
        elif s[0] == "y":
            b = take("y" + t)
            op("P", lambda: P.matmul(T[b][0:8, :], T.CW[:, :], buf("A" + t), True, True), ["CW"] + hk("A" + t), [b])
        elif s[0] == "Y":
            b = give("y" + t)
            act(T.yas[0:8, int(t) * E:(int(t) + 1) * E], T[b][0:8, :], AF.Identity, [b], ["yas" + t])
        elif s == "dy":
            dma("S", "dya", T.ya[:, :], T.yas[0:8, :], ["yas0", "yas1"], [])
        elif s[0] == "f":
            b = "ps%d" % (int(x) % 2)
            op("P", lambda: P.matmul(T[b][:, 0:32], T.I16[:, :], T.FR[:, :], True, False), ["I16", "FR"], [b])
        elif s[0] == "G":
            tab, name, mask = "RW" if int(x) % 2 else "LW", "v" + t if x == "1" else "x%d" % (int(x) - 1), ("A" if int(x) % 2 else "B") + t
            op("V", lambda: V.tensor_tensor(buf("G" + x), gat(tab, name), buf(mask), ALU.mult), TAB[tab] + lk(name) + hk(mask), hk("G" + x))
        elif s[0] == "l":
            b = "ps%d" % (int(x) % 2)
            for j in range(16):
                a = 15 - j if j % 2 else 160 - j
                op("P", lambda: P.matmul(T[b][:, 0:32], T.Z[:, a:a + 128], T["G" + x][:, j:E:16], False, j == 15), ["Z0", "Z1"] + hk("G" + x), [b])
        elif s[0] == "c":
            cp(offs("x" + x), T["ps%d" % (int(x) % 2)][:, 0:32], ["ps%d" % (int(x) % 2)], ["lx" + x])
        elif s[0] == "m":
            spare(int(s[3]), t)
        elif s[0] == "k":
            name = "u" + t if x == "u" else "x" + x
            if h == 1:
                cp(buf("col" + x, h), gat("LW", name, h), TAB["LW"] + lk(name), hk("col" + x, h))
            else:
                act(buf("col" + x, h), gat("LW", name, h), AF.Identity, TAB["LW"] + lk(name), hk("col" + x, h))
        elif s[0] == "P":
            if t == "0" and x in "135":
                withps("P" + x, "m0" + x, "D", ALU.mult)
            else:
                fromps("P" + x, "m" + t + x, bias=W - BIG if x in "u5" else -BIG)
        elif s[0] == "s":
            name, alu = "u" + t if x == "u" else "y" + x, ALU.add if t == "0" and x != "u" else ALU.subtract
            op("V", lambda: V.tensor_tensor(sca("LW", name, h), buf("col" + x, h), buf("P" + x, h), alu),
               hk("col" + x, h) + hk("P" + x, h) + lk(name), TAB["LW"])
        elif s[0] == "w":
            op("V", lambda: V.tensor_tensor(buf(s), gat("RW", "x" + t), buf("P" + t), ALU.subtract), TAB["RW"] + lk("x" + t) + hk("P" + t), hk(s))
        elif s[0] == "z":
            act(buf(s), buf("w" + t), AF.Abs, hk("w" + t), hk(s))
        else:
            name = "v0" if t == "0" else "y" + t
            op("A", lambda: A.activation(sca("RW", name, h), buf("z" + t, h), AF.Silu), hk("z" + t, h) + lk(name), TAB["RW"])

    for s in ORDER[(far_out, far_in)].split():
        do(s)

    for k in range(NO):
        a, b = OCH[k], OCH[k + 1]
        act(T.outb[:, a:b], T.LW[:, a:b], AF.Abs, TAB["LW"], ["outb%d" % k])
        dma("S", "dout%d" % k, T.yl[:, a:b], T.outb[:, a:b], ["outb%d" % k], [])
    for s, c in total.items():
        need("G" if s == "sent" else "S", (s, c, {}))
